import numpy as np
import ml_dtypes


def mxq(x, axis, fmt="e4m3"):
    dtype, down = {"e4m3": (ml_dtypes.float8_e4m3fn, 7), "e5m2": (ml_dtypes.float8_e5m2, 14)}[fmt]
    v = np.moveaxis(np.asarray(x, np.float32).astype(ml_dtypes.bfloat16).astype(np.float64), axis, -1)
    blocks = v.reshape(v.shape[:-1] + (-1, 32))
    amax = np.abs(blocks).max(-1, keepdims=True)
    byte = np.maximum(np.where(amax > 0, np.frexp(amax)[1] - 1 + 127, 0) - down, 1)
    scale = np.exp2(byte - 127.0)
    codes = (blocks / scale).astype(np.float32).astype(dtype).astype(np.float64)
    return np.moveaxis((codes * scale).reshape(v.shape), -1, axis)


WIDE = False


def mx_kscale(k):
    if not WIDE:
        return np.ones(k)
    levels = np.array([10, -10, 5, -5, 0])
    if k % 512:
        return np.exp2(np.random.permutation(np.resize(levels, k // 32))).repeat(32)
    a = np.empty((k // 512, 16))
    for p in range(k // 512):
        a[p, :8] = np.random.permutation(np.resize(levels, 8))
        for g in range(8):
            far = levels[np.abs(levels - a[p, g]) >= 10]
            a[p, g + 8] = far[np.random.randint(len(far))]
    return np.exp2(a.ravel()).repeat(32)


BF16 = ml_dtypes.bfloat16


def bf(x):
    return np.asarray(x, np.float32).astype(BF16)


def f64(x):
    return np.asarray(x).astype(np.float64)


E2M1 = np.array([0.0, 0.5, 1.0, 1.5, 2.0, 3.0, 4.0, 6.0, -0.0, -0.5, -1.0, -1.5, -2.0, -3.0, -4.0, -6.0])


def pack_weight(w, fmt):
    k, n = w.shape
    w = f64(bf(w)).reshape(k // 32, 32, n)
    amax = np.abs(w).max(1)
    if fmt == "e4m3":
        byte = np.frexp(amax)[1] - 1 + 127 - 7
    else:
        mant, ex = np.frexp(amax / 6.0)
        byte = np.where(mant > 0.5, ex, ex - 1) + 127
    byte = np.clip(np.where(amax > 0, byte, 1), 1, 254)
    scaled = (w * np.exp2(127.0 - byte)[:, None, :]).reshape(k, n).astype(np.float32)
    by_word = np.ascontiguousarray(scaled.reshape(k // 512, 128, 4, n).transpose(0, 1, 3, 2))
    if fmt == "e4m3":
        words = by_word.astype(ml_dtypes.float8_e4m3fn).view(np.uint8)
    else:
        c = by_word.astype(ml_dtypes.float4_e2m1fn).view(np.uint8) & 0xF
        words = c[..., 0::2] | (c[..., 1::2] << 4)
    return np.ascontiguousarray(words), np.ascontiguousarray(byte.astype(np.uint8).reshape(k // 512, 16, n))


def unpack_weight(words, scales, fmt):
    g, p, n, _ = words.shape
    if fmt == "e4m3":
        vals = np.ascontiguousarray(words).view(ml_dtypes.float8_e4m3fn).astype(np.float64)
    else:
        nib = np.empty((g, p, n, 4), np.uint8)
        nib[..., 0::2] = words & 0xF
        nib[..., 1::2] = words >> 4
        vals = E2M1[nib]
    vals = vals * np.repeat(np.exp2(scales.astype(np.float64) - 127.0), 8, axis=1)[..., None]
    return vals.transpose(0, 1, 3, 2).reshape(g * 512, n)
def pack4(w):
    words, scales = pack_weight(w, "e2m1")
    return words.reshape(words.shape[0], 128, -1), scales


def unpack4(words, scales):
    return unpack_weight(words.reshape(words.shape[0], 128, -1, 2), scales, "e2m1")


E4M3FN = np.array([(-1.0 if i & 128 else 1.0) * ((1.0 + (i & 7) / 8.0) * 2.0 ** (((i >> 3) & 15) - 7) if i & 120 else (i & 7) * 2.0 ** -9) for i in range(256)])


def e4m3fn_bytes(y):
    return np.clip(np.asarray(y, np.float64), -448.0, 448.0).astype(np.float32).astype(ml_dtypes.float8_e4m3fn).view(np.uint8)


def e4m3fn_values(b):
    return E4M3FN[b]


T, K, V, P, B = 3072, 1024, 512, 1536, 128


def setup_inputs():
    s, t = mx_kscale(K), mx_kscale(T)
    x = np.random.standard_normal((T, K)) * s
    x_scale = (np.abs(x).reshape(T, K // B, B).max(axis=2) / 448.0).astype(np.float32)
    x_bytes = e4m3fn_bytes(x / np.repeat(f64(x_scale), B, axis=1))
    e_words, e_scales = pack4(np.random.standard_normal((T, P)) / np.sqrt(T) / t[:, None])
    return {"x_bytes": x_bytes,
            "x_scale": x_scale,
            "c": bf(np.random.standard_normal((K, V)) / np.sqrt(K) / s[:, None]),
            "o": bf(0.4 * np.random.standard_normal(V)),
            "w": bf(np.random.uniform(0.5, 1.5, (T, V)) * t[:, None]),
            "e_words": e_words,
            "e_scales": e_scales}


def reference(x_bytes, x_scale, c, o, w, e_words, e_scales):
    x = e4m3fn_values(x_bytes) * np.repeat(f64(x_scale), B, axis=1)
    y = mxq(x, 1, "e4m3") @ mxq(f64(c), 0, "e4m3")
    h = (y - f64(o)) * f64(w)
    z = mxq(h, 0, "e4m3").T @ unpack4(e_words, e_scales)
    return z

@@ -1,0 +1,361 @@
+from contextlib import ExitStack
+
+import concourse.mybir as mybir
+from concourse.masks import make_identity
+
+T, K, V, G = 3072, 1024, 512, 1536
+FLOPS = 2 * T * K * V + 2 * V * T * G
+
+F32 = mybir.dt.float32
+BF16 = mybir.dt.bfloat16
+I32 = mybir.dt.int32
+U32 = mybir.dt.uint32
+U8 = mybir.dt.uint8
+FP8 = mybir.dt.float8_e4m3fn
+FP8X4 = mybir.dt.float8_e4m3fn_x4
+FP4X4 = mybir.dt.float4_e2m1fn_x4
+MULT = mybir.AluOpType.mult
+SUBTRACT = mybir.AluOpType.subtract
+COPY = mybir.ActivationFunctionType.Copy
+
+P = 128
+PACK = 4
+PASS = P * PACK
+GROUPS = T // PASS
+K_PASSES = K // PASS
+BLOCK = 128
+BLOCKS = K // BLOCK
+HALF = V // 2
+BANK = 512
+WIDE_BUFS = 8
+TURNED_BUFS = 3
+OUT_BUFS = 6
+VECTOR_BLOCKS = [[5, 5, 5, 5], [5, 5, 5, 5], [4, 5, 4, 5], [3, 4, 3, 4], [3, 4, 3, 4], [3, 4, 3, 4]]
+
+
+def tile_coil_compress_regrid_d4_kernel(tc, x_bytes, x_scale, c, o, w, e_words, e_scales, out):
+    nc = tc.nc
+    with ExitStack() as ctx:
+        sb = ctx.enter_context(tc.tile_pool(name="sb", bufs=1))
+        ps = ctx.enter_context(tc.psum_pool(name="ps", bufs=1))
+        ctx.enter_context(tc.manual_schedule())
+
+        def ring(count, shape, dtype, name):
+            return [sb.tile(shape, dtype, name="%s%d" % (name, i), align_bytes=64) for i in range(count)]
+
+        x_raw = ring(GROUPS, [P, PACK * K], U8, "x_raw")
+        x_factor = sb.tile([P, GROUPS, PACK * BLOCKS], F32, name="x_factor")
+        c_raw = sb.tile([P, K_PASSES, PACK, V], BF16, name="c_raw")
+        c_grouped = ring(2, [P, K_PASSES, HALF, PACK], BF16, "c_grouped")
+        c_codes = ring(2, [P, K_PASSES * HALF], U32, "c_codes")
+        c_exps = ring(2, [P, K_PASSES * HALF], U8, "c_exps")
+        w_raw = ring(GROUPS, [P, PACK, V], BF16, "w_raw")
+        e_codes = ring(GROUPS, [P, 2 * G], U8, "e_codes")
+        e_exps = sb.tile([P, GROUPS, G], U8, name="e_exps", align_bytes=64)
+        o_row = sb.tile([P, V], BF16, name="o_row")
+        ones = sb.tile([P, P], BF16, name="ones")
+        o_all = sb.tile([P, V], F32, name="o_all")
+        ident = sb.tile([P, P], F32, name="ident")
+        x_wide = ring(WIDE_BUFS, [P, K], BF16, "x_wide")
+        x_turned = ring(TURNED_BUFS, [P, 2 * K], BF16, "x_turned")
+        x_codes = ring(2 * GROUPS, [P, 2 * K // PACK], U32, "x_codes")
+        x_exps = ring(2 * GROUPS, [P, 2 * K // PACK], U8, "x_exps")
+        shifted = ring(2, [P, PACK, HALF], F32, "shifted")
+        h_grouped = ring(2, [P, HALF, PACK], BF16, "h_grouped")
+        h_codes = ring(2 * GROUPS, [P, HALF], U32, "h_codes")
+        h_exps = ring(2 * GROUPS, [P, HALF], U8, "h_exps")
+        z_stage = ring(OUT_BUFS, [P, BANK], F32, "z_stage")
+        banks = [ps.tile([P, BANK], F32, name="bank%d" % i) for i in range(8)]
+        sums, stream = banks[:4], banks[4:]
+
+        x_rows = x_bytes.rearrange("(g p t) k -> g p (t k)", p=P, t=PACK)
+        w_rows = w.rearrange("(g p t) v -> g p t v", p=P, t=PACK)
+        c_rows = c.rearrange("(s p j) v -> s p j v", p=P, j=PACK)
+
+        def load_x(g):
+            nc.sync.dma_start(out=x_raw[g][:], in_=x_rows[g])
+
+        def load_w(g):
+            nc.sync.dma_start(out=w_raw[g][:], in_=w_rows[g])
+
+        def load_e(g):
+            nc.sync.dma_start(out=e_codes[g][:].bitcast(I32), in_=e_words[g].bitcast(I32))
+
+        nc.vector.memset(o_row[:], 0.0)
+        nc.vector.memset(ones[:], 0.0)
+        nc.vector.memset(e_exps[:].rearrange("p g n -> p (g n)").bitcast(I32), 0)
+        nc.scalar.activation(out=ones[:], in_=ones[:], func=COPY, bias=1.0)
+        make_identity(nc, ident[:])
+
+        nc.sync.dma_start(out=x_raw[0][:, : 2 * K], in_=x_rows[0][:, : 2 * K])
+        nc.sync.dma_start(out=x_factor[:], in_=x_scale.rearrange("(g p t) b -> p g (t b)", p=P, t=PACK))
+        nc.sync.dma_start(out=o_row[0:1, :], in_=o.rearrange("(a v) -> a v", a=1))
+        nc.sync.dma_start(out=x_raw[0][:, 2 * K :], in_=x_rows[0][:, 2 * K :])
+        load_x(1)
+        for s in range(K_PASSES):
+            nc.sync.dma_start(out=c_raw[:, s], in_=c_rows[s])
+        load_x(2)
+        load_x(3)
+        load_w(0)
+        for q in range(4):
+            nc.sync.dma_start(
+                out=e_exps[32 * q : 32 * q + 4].bitcast(I32),
+                in_=e_scales[:, 4 * q : 4 * q + 4, :].bitcast(I32).rearrange("g r n -> r g n"),
+            )
+        load_e(0)
+        load_x(4)
+        load_w(1)
+        load_e(1)
+        load_x(5)
+        for g in range(2, GROUPS):
+            load_w(g)
+            load_e(g)
+
+        def widen_block(g, t, b, on_vector):
+            src = x_raw[g][:, t * K + b * BLOCK : t * K + (b + 1) * BLOCK].bitcast(FP8)
+            dst = x_wide[(PACK * g + t) % WIDE_BUFS][:, b * BLOCK : (b + 1) * BLOCK]
+            factor = x_factor[:, g, t * BLOCKS + b : t * BLOCKS + b + 1]
+            if on_vector:
+                nc.vector.tensor_scalar(out=dst, in0=src, scalar1=factor, scalar2=None, op0=MULT)
+            else:
+                nc.scalar.activation(out=dst, in_=src, func=COPY, scale=factor)
+
+        def widen_vector(g, t):
+            if g < GROUPS:
+                for b in range(VECTOR_BLOCKS[g][t]):
+                    widen_block(g, t, b, True)
+
+        def widen_scalar(g, t):
+            if g < GROUPS:
+                for b in range(VECTOR_BLOCKS[g][t], BLOCKS):
+                    widen_block(g, t, b, False)
+
+        def turn(g, t, bank):
+            words = x_wide[(PACK * g + t) % WIDE_BUFS][:].bitcast(F32)
+            for s in range(K_PASSES):
+                for u in range(2):
+                    col = (2 * s + u) * P
+                    nc.tensor.transpose(bank[:, col : col + P], words[:, 2 * P * s + u : 2 * P * (s + 1) : 2], ident[:])
+
+        def empty_turned(g, t, bank):
+            dst = x_turned[(2 * g + t // 2) % TURNED_BUFS][:, (t % 2) * K : (t % 2 + 1) * K].bitcast(F32)
+            nc.scalar.copy(
+                out=dst.rearrange("p (s r u) -> p s r u", s=K_PASSES, u=2),
+                in_=bank[:].rearrange("p (s u r) -> p s r u", s=K_PASSES, u=2),
+            )
+
+        def quantize_x(g, pair):
+            n = 2 * g + pair
+            nc.vector.quantize_mx(out=x_codes[n][:].bitcast(FP8X4), scales=x_exps[n][:], in_=x_turned[n % TURNED_BUFS][:])
+
+        def group_c(half, s, on_vector):
+            src = c_raw[:, s, :, half * HALF : (half + 1) * HALF].rearrange("p j v -> p v j")
+            if on_vector:
+                nc.vector.tensor_copy(out=c_grouped[half][:, s], in_=src)
+            else:
+                nc.scalar.copy(out=c_grouped[half][:, s], in_=src)
+
+        def quantize_c(half):
+            nc.vector.quantize_mx(
+                out=c_codes[half][:].bitcast(FP8X4),
+                scales=c_exps[half][:],
+                in_=c_grouped[half][:].rearrange("p s v j -> p (s v j)"),
+            )
+
+        def compress(g, half, pair, bank):
+            n = 2 * g + pair
+            for slot in range(2):
+                for s in range(K_PASSES):
+                    cols = slice((slot * K_PASSES + s) * P, (slot * K_PASSES + s + 1) * P)
+                    c_cols = slice(s * HALF, (s + 1) * HALF)
+                    nc.tensor.matmul_mx(
+                        out=bank[:, slot * HALF : (slot + 1) * HALF],
+                        lhsT=x_codes[n][:, cols].bitcast(FP8X4),
+                        lhsT_scale=x_exps[n][:, cols],
+                        rhs=c_codes[half][:, c_cols].bitcast(FP8X4),
+                        rhs_scale=c_exps[half][:, c_cols],
+                        start=(s == 0),
+                        stop=(s == K_PASSES - 1),
+                    )
+
+        def shift(g, half, pair, bank):
+            offset = o_all[:, half * HALF : (half + 1) * HALF].unsqueeze(1).to_broadcast([P, 2, HALF])
+            nc.vector.tensor_tensor(
+                out=shifted[g % 2][:, 2 * pair : 2 * pair + 2, :],
+                in0=bank[:].rearrange("p (t v) -> p t v", t=2),
+                in1=offset,
+                op=SUBTRACT,
+            )
+
+        def weigh(g, half):
+            nc.vector.tensor_tensor(
+                out=h_grouped[g % 2][:],
+                in0=shifted[g % 2][:].rearrange("p t v -> p v t"),
+                in1=w_raw[g][:, :, half * HALF : (half + 1) * HALF].rearrange("p t v -> p v t"),
+                op=MULT,
+            )
+
+        def quantize_h(g, half):
+            n = 2 * g + half
+            nc.vector.quantize_mx(
+                out=h_codes[n][:].bitcast(FP8X4),
+                scales=h_exps[n][:],
+                in_=h_grouped[g % 2][:].rearrange("p v t -> p (v t)"),
+            )
+
+        def regrid(g, row, col, bank):
+            n = 2 * g + row // 2
+            cols = slice((row % 2) * P, (row % 2 + 1) * P)
+            nc.tensor.matmul_mx(
+                out=bank[:],
+                lhsT=h_codes[n][:, cols].bitcast(FP8X4),
+                lhsT_scale=h_exps[n][:, cols],
+                rhs=e_codes[g][:, 2 * col * BANK : 2 * (col + 1) * BANK].bitcast(FP4X4),
+                rhs_scale=e_exps[:, g, col * BANK : (col + 1) * BANK],
+                start=(g == 0),
+                stop=(g == GROUPS - 1),
+            )
+
+        stored = []
+
+        def store(row, col, bank, on_vector):
+            stage = z_stage[len(stored) % OUT_BUFS]
+            stored.append((row, col))
+            if on_vector:
+                nc.vector.tensor_copy(out=stage[:], in_=bank[:])
+            else:
+                nc.scalar.copy(out=stage[:], in_=bank[:])
+            nc.sync.dma_start(out=out[row * P : (row + 1) * P, col * BANK : (col + 1) * BANK], in_=stage[:])
+
+        taken = []
+
+        def next_bank():
+            taken.append(0)
+            return stream[(len(taken) - 1) % len(stream)]
+
+        early = [(0, 0, sums[0]), (0, 1, sums[1]), (1, 0, sums[2]), (1, 1, sums[3])]
+
+        nc.tensor.matmul(out=sums[0][:], lhsT=ones[:], rhs=o_row[:], start=True, stop=True)
+        for t in range(PACK):
+            widen_vector(0, t)
+            widen_scalar(0, t)
+        nc.scalar.copy(out=o_all[:], in_=sums[0][:])
+
+        for g in range(-1, GROUPS - 1):
+            turned = [next_bank() for t in range(PACK)]
+            if g >= 0:
+                quantize_x(g, 1)
+            if g == 0:
+                quantize_c(0)
+            turn(g + 1, 0, turned[0])
+            widen_scalar(g + 2, 0)
+            if g >= 1:
+                weigh(g - 1, 0)
+            empty_turned(g + 1, 0, turned[0])
+            turn(g + 1, 1, turned[1])
+            widen_vector(g + 2, 0)
+            if g >= 1:
+                quantize_h(g - 1, 0)
+            widen_scalar(g + 2, 1)
+            empty_turned(g + 1, 1, turned[1])
+            widen_vector(g + 2, 1)
+            turn(g + 1, 2, turned[2])
+            turn(g + 1, 3, turned[3])
+            quantize_x(g + 1, 0)
+            if g >= 0:
+                made = [next_bank(), next_bank()]
+                compress(g, 0, 0, made[0])
+                compress(g, 0, 1, made[1])
+            widen_scalar(g + 2, 2)
+            empty_turned(g + 1, 2, turned[2])
+            widen_vector(g + 2, 2)
+            if g >= 0:
+                shift(g, 0, 0, made[0])
+                shift(g, 0, 1, made[1])
+            widen_scalar(g + 2, 3)
+            empty_turned(g + 1, 3, turned[3])
+            widen_vector(g + 2, 3)
+            if g == -1:
+                group_c(0, 0, True)
+                group_c(0, 1, True)
+            if g == GROUPS - 2:
+                group_c(1, 0, False)
+                group_c(1, 1, False)
+            if g >= 1:
+                for row, col, bank in early:
+                    regrid(g - 1, row, col, bank)
+
+        last = GROUPS - 1
+        odd, even = stream[2:], stream[:2]
+
+        def compress_both(g, half, pair_banks):
+            compress(g, half, 0, pair_banks[0])
+            compress(g, half, 1, pair_banks[1])
+
+        def shift_both(g, half, pair_banks):
+            shift(g, half, 0, pair_banks[0])
+            shift(g, half, 1, pair_banks[1])
+
+        def regrid_all(g, tiles):
+            for row, col, bank in tiles:
+                regrid(g, row, col, bank)
+
+        quantize_x(last, 1)
+        weigh(last - 1, 0)
+        quantize_c(1)
+        quantize_h(last - 1, 0)
+        compress_both(last, 0, odd)
+        compress_both(0, 1, even)
+        regrid_all(last - 1, early)
+        shift_both(last, 0, odd)
+        weigh(last, 0)
+        compress_both(1, 1, odd)
+        shift(0, 1, 0, even[0])
+        quantize_h(last, 0)
+        shift(0, 1, 1, even[1])
+        for row, col, bank in early:
+            regrid(last, row, col, bank)
+            store(row, col, bank, False)
+        weigh(0, 1)
+        compress_both(2, 1, even)
+        shift_both(1, 1, odd)
+        quantize_h(0, 1)
+        weigh(1, 1)
+        for row in range(2):
+            for g in range(GROUPS):
+                regrid(g, row, 2, sums[row])
+            store(row, 2, sums[row], False)
+        compress_both(3, 1, odd)
+        shift_both(2, 1, even)
+        quantize_h(1, 1)
+        weigh(2, 1)
+        first_col = [(2, 0, sums[2]), (3, 0, sums[3])]
+        second_col = [(2, 1, sums[0]), (3, 1, sums[1])]
+        third_col = [(2, 2, odd[0]), (3, 2, odd[1])]
+        for tiles in (first_col, second_col):
+            regrid_all(0, tiles)
+            regrid_all(1, tiles)
+        compress_both(4, 1, even)
+        shift_both(3, 1, odd)
+        quantize_h(2, 1)
+        weigh(3, 1)
+        regrid_all(2, first_col + second_col)
+        shift_both(4, 1, even)
+        quantize_h(3, 1)
+        weigh(4, 1)
+        compress_both(5, 1, even)
+        regrid_all(3, first_col + second_col)
+        shift_both(5, 1, even)
+        quantize_h(4, 1)
+        weigh(5, 1)
+        quantize_h(5, 1)
+        regrid_all(4, first_col + second_col)
+        for g in range(3):
+            regrid_all(g, third_col)
+        for i, (row, col, bank) in enumerate(first_col + second_col):
+            regrid(last, row, col, bank)
+            store(row, col, bank, i % 2 == 1)
+        for i, (row, col, bank) in enumerate(third_col):
+            for g in range(3, GROUPS):
+                regrid(g, row, col, bank)
+            store(row, col, bank, i % 2 == 1)

@@ -30,7 +30,7 @@ BANK = 512
 WIDE_BUFS = 8
 TURNED_BUFS = 3
 OUT_BUFS = 6
-VECTOR_BLOCKS = [[5, 5, 5, 5], [5, 5, 5, 5], [4, 5, 4, 5], [3, 4, 3, 4], [3, 4, 3, 4], [3, 4, 3, 4]]
+VECTOR_BLOCKS = [[5, 5, 5, 5], [6, 6, 6, 6], [4, 5, 4, 5], [3, 4, 3, 4], [3, 4, 3, 4], [3, 4, 3, 4]]
 
 
 def tile_coil_compress_regrid_d4_kernel(tc, x_bytes, x_scale, c, o, w, e_words, e_scales, out):
@@ -45,7 +45,7 @@ def tile_coil_compress_regrid_d4_kernel(tc, x_bytes, x_scale, c, o, w, e_words, 
 
         x_raw = ring(GROUPS, [P, PACK * K], U8, "x_raw")
         x_factor = sb.tile([P, GROUPS, PACK * BLOCKS], F32, name="x_factor")
-        c_raw = sb.tile([P, K_PASSES, PACK, V], BF16, name="c_raw")
+        c_raw = ring(2, [P, K_PASSES, PACK, HALF], BF16, "c_raw")
         c_grouped = ring(2, [P, K_PASSES, HALF, PACK], BF16, "c_grouped")
         c_codes = ring(2, [P, K_PASSES * HALF], U32, "c_codes")
         c_exps = ring(2, [P, K_PASSES * HALF], U8, "c_exps")
@@ -78,6 +78,10 @@ def tile_coil_compress_regrid_d4_kernel(tc, x_bytes, x_scale, c, o, w, e_words, 
         def load_w(g):
             nc.sync.dma_start(out=w_raw[g][:], in_=w_rows[g])
 
+        def load_c(half):
+            for s in range(K_PASSES):
+                nc.sync.dma_start(out=c_raw[half][:, s], in_=c_rows[s][:, :, half * HALF : (half + 1) * HALF])
+
         def load_e(g):
             nc.sync.dma_start(out=e_codes[g][:].bitcast(I32), in_=e_words[g].bitcast(I32))
 
@@ -91,12 +95,11 @@ def tile_coil_compress_regrid_d4_kernel(tc, x_bytes, x_scale, c, o, w, e_words, 
         nc.sync.dma_start(out=x_factor[:], in_=x_scale.rearrange("(g p t) b -> p g (t b)", p=P, t=PACK))
         nc.sync.dma_start(out=o_row[0:1, :], in_=o.rearrange("(a v) -> a v", a=1))
         nc.sync.dma_start(out=x_raw[0][:, 2 * K :], in_=x_rows[0][:, 2 * K :])
+        load_c(0)
         load_x(1)
-        for s in range(K_PASSES):
-            nc.sync.dma_start(out=c_raw[:, s], in_=c_rows[s])
         load_x(2)
-        load_x(3)
         load_w(0)
+        load_x(3)
         for q in range(4):
             nc.sync.dma_start(
                 out=e_exps[32 * q : 32 * q + 4].bitcast(I32),
@@ -107,6 +110,7 @@ def tile_coil_compress_regrid_d4_kernel(tc, x_bytes, x_scale, c, o, w, e_words, 
         load_w(1)
         load_e(1)
         load_x(5)
+        load_c(1)
         for g in range(2, GROUPS):
             load_w(g)
             load_e(g)
@@ -149,11 +153,12 @@ def tile_coil_compress_regrid_d4_kernel(tc, x_bytes, x_scale, c, o, w, e_words, 
             nc.vector.quantize_mx(out=x_codes[n][:].bitcast(FP8X4), scales=x_exps[n][:], in_=x_turned[n % TURNED_BUFS][:])
 
         def group_c(half, s, on_vector):
-            src = c_raw[:, s, :, half * HALF : (half + 1) * HALF].rearrange("p j v -> p v j")
+            src = c_raw[half][:, s].rearrange("p j (a b) -> p a j b", b=PACK)
+            dst = c_grouped[half][:, s].rearrange("p (a b) j -> p a j b", b=PACK)
             if on_vector:
-                nc.vector.tensor_copy(out=c_grouped[half][:, s], in_=src)
+                nc.vector.tensor_copy(out=dst, in_=src)
             else:
-                nc.scalar.copy(out=c_grouped[half][:, s], in_=src)
+                nc.scalar.copy(out=dst, in_=src)
 
         def quantize_c(half):
             nc.vector.quantize_mx(
@@ -189,9 +194,9 @@ def tile_coil_compress_regrid_d4_kernel(tc, x_bytes, x_scale, c, o, w, e_words, 
 
         def weigh(g, half):
             nc.vector.tensor_tensor(
-                out=h_grouped[g % 2][:],
-                in0=shifted[g % 2][:].rearrange("p t v -> p v t"),
-                in1=w_raw[g][:, :, half * HALF : (half + 1) * HALF].rearrange("p t v -> p v t"),
+                out=h_grouped[g % 2][:].rearrange("p (a b) t -> p a t b", b=PACK),
+                in0=shifted[g % 2][:].rearrange("p t (a b) -> p a t b", b=PACK),
+                in1=w_raw[g][:, :, half * HALF : (half + 1) * HALF].rearrange("p t (a b) -> p a t b", b=PACK),
                 op=MULT,
             )
 
@@ -235,59 +240,6 @@ def tile_coil_compress_regrid_d4_kernel(tc, x_bytes, x_scale, c, o, w, e_words, 
 
         early = [(0, 0, sums[0]), (0, 1, sums[1]), (1, 0, sums[2]), (1, 1, sums[3])]
 
-        nc.tensor.matmul(out=sums[0][:], lhsT=ones[:], rhs=o_row[:], start=True, stop=True)
-        for t in range(PACK):
-            widen_vector(0, t)
-            widen_scalar(0, t)
-        nc.scalar.copy(out=o_all[:], in_=sums[0][:])
-
-        for g in range(-1, GROUPS - 1):
-            turned = [next_bank() for t in range(PACK)]
-            if g >= 0:
-                quantize_x(g, 1)
-            if g == 0:
-                quantize_c(0)
-            turn(g + 1, 0, turned[0])
-            widen_scalar(g + 2, 0)
-            if g >= 1:
-                weigh(g - 1, 0)
-            empty_turned(g + 1, 0, turned[0])
-            turn(g + 1, 1, turned[1])
-            widen_vector(g + 2, 0)
-            if g >= 1:
-                quantize_h(g - 1, 0)
-            widen_scalar(g + 2, 1)
-            empty_turned(g + 1, 1, turned[1])
-            widen_vector(g + 2, 1)
-            turn(g + 1, 2, turned[2])
-            turn(g + 1, 3, turned[3])
-            quantize_x(g + 1, 0)
-            if g >= 0:
-                made = [next_bank(), next_bank()]
-                compress(g, 0, 0, made[0])
-                compress(g, 0, 1, made[1])
-            widen_scalar(g + 2, 2)
-            empty_turned(g + 1, 2, turned[2])
-            widen_vector(g + 2, 2)
-            if g >= 0:
-                shift(g, 0, 0, made[0])
-                shift(g, 0, 1, made[1])
-            widen_scalar(g + 2, 3)
-            empty_turned(g + 1, 3, turned[3])
-            widen_vector(g + 2, 3)
-            if g == -1:
-                group_c(0, 0, True)
-                group_c(0, 1, True)
-            if g == GROUPS - 2:
-                group_c(1, 0, False)
-                group_c(1, 1, False)
-            if g >= 1:
-                for row, col, bank in early:
-                    regrid(g - 1, row, col, bank)
-
-        last = GROUPS - 1
-        odd, even = stream[2:], stream[:2]
-
         def compress_both(g, half, pair_banks):
             compress(g, half, 0, pair_banks[0])
             compress(g, half, 1, pair_banks[1])
@@ -300,42 +252,103 @@ def tile_coil_compress_regrid_d4_kernel(tc, x_bytes, x_scale, c, o, w, e_words, 
             for row, col, bank in tiles:
                 regrid(g, row, col, bank)
 
+        nc.tensor.matmul(out=sums[0][:], lhsT=ones[:], rhs=o_row[:], start=True, stop=True)
+        for t in range(PACK):
+            widen_vector(0, t)
+            widen_scalar(0, t)
+
+        turned = [next_bank() for t in range(PACK)]
+        group_c(0, 0, True)
+        group_c(0, 1, True)
+        for t in range(PACK):
+            turn(0, t, turned[t])
+            empty_turned(0, t, turned[t])
+            widen_vector(1, t)
+            if t == 0:
+                quantize_c(0)
+            if t == 1:
+                quantize_x(0, 0)
+            if t >= 1:
+                widen_scalar(1, t - 1)
+        nc.scalar.copy(out=o_all[:], in_=sums[0][:])
+        widen_scalar(1, 3)
+
+        for g in range(GROUPS - 1):
+            turned = [next_bank() for t in range(PACK)]
+            quantize_x(g, 1)
+            turn(g + 1, 0, turned[0])
+            widen_scalar(g + 2, 0)
+            if g == GROUPS - 2:
+                group_c(1, 0, False)
+            if g >= 1:
+                weigh(g - 1, 0)
+            empty_turned(g + 1, 0, turned[0])
+            turn(g + 1, 1, turned[1])
+            widen_vector(g + 2, 0)
+            if g == GROUPS - 2:
+                group_c(1, 1, True)
+            if g >= 1:
+                quantize_h(g - 1, 0)
+            widen_scalar(g + 2, 1)
+            empty_turned(g + 1, 1, turned[1])
+            widen_vector(g + 2, 1)
+            turn(g + 1, 2, turned[2])
+            turn(g + 1, 3, turned[3])
+            quantize_x(g + 1, 0)
+            made = [next_bank(), next_bank()]
+            compress_both(g, 0, made)
+            widen_scalar(g + 2, 2)
+            empty_turned(g + 1, 2, turned[2])
+            widen_vector(g + 2, 2)
+            if g == GROUPS - 2:
+                quantize_c(1)
+            shift_both(g, 0, made)
+            widen_scalar(g + 2, 3)
+            empty_turned(g + 1, 3, turned[3])
+            widen_vector(g + 2, 3)
+            if g >= 1:
+                regrid_all(g - 1, early)
+
+        last = GROUPS - 1
+        odd, even = stream[2:], stream[:2]
+
         quantize_x(last, 1)
         weigh(last - 1, 0)
-        quantize_c(1)
-        quantize_h(last - 1, 0)
         compress_both(last, 0, odd)
+        shift(last, 0, 0, odd[0])
+        quantize_h(last - 1, 0)
         compress_both(0, 1, even)
+        shift(last, 0, 1, odd[1])
         regrid_all(last - 1, early)
-        shift_both(last, 0, odd)
+        shift(0, 1, 0, even[0])
         weigh(last, 0)
         compress_both(1, 1, odd)
-        shift(0, 1, 0, even[0])
-        quantize_h(last, 0)
         shift(0, 1, 1, even[1])
+        quantize_h(last, 0)
+        compress_both(2, 1, even)
         for row, col, bank in early:
             regrid(last, row, col, bank)
             store(row, col, bank, False)
         weigh(0, 1)
-        compress_both(2, 1, even)
         shift_both(1, 1, odd)
         quantize_h(0, 1)
         weigh(1, 1)
+        compress_both(3, 1, odd)
         for row in range(2):
             for g in range(GROUPS):
                 regrid(g, row, 2, sums[row])
             store(row, 2, sums[row], False)
-        compress_both(3, 1, odd)
         shift_both(2, 1, even)
         quantize_h(1, 1)
         weigh(2, 1)
         first_col = [(2, 0, sums[2]), (3, 0, sums[3])]
         second_col = [(2, 1, sums[0]), (3, 1, sums[1])]
         third_col = [(2, 2, odd[0]), (3, 2, odd[1])]
-        for tiles in (first_col, second_col):
-            regrid_all(0, tiles)
-            regrid_all(1, tiles)
+        regrid_all(0, first_col)
+        regrid_all(1, first_col)
         compress_both(4, 1, even)
+        regrid_all(0, second_col)
+        regrid_all(1, second_col)
         shift_both(3, 1, odd)
         quantize_h(2, 1)
         weigh(3, 1)
@@ -349,9 +362,9 @@ def tile_coil_compress_regrid_d4_kernel(tc, x_bytes, x_scale, c, o, w, e_words, 
         quantize_h(4, 1)
         weigh(5, 1)
         quantize_h(5, 1)
-        regrid_all(4, first_col + second_col)
         for g in range(3):
             regrid_all(g, third_col)
+        regrid_all(4, first_col + second_col)
         for i, (row, col, bank) in enumerate(first_col + second_col):
             regrid(last, row, col, bank)
             store(row, col, bank, i % 2 == 1)

@@ -30,7 +30,7 @@ BANK = 512
 WIDE_BUFS = 8
 TURNED_BUFS = 3
 OUT_BUFS = 6
-VECTOR_BLOCKS = [[5, 5, 5, 5], [6, 6, 6, 6], [4, 5, 4, 5], [3, 4, 3, 4], [3, 4, 3, 4], [3, 4, 3, 4]]
+VECTOR_BLOCKS = [[5, 5, 5, 5], [6, 6, 6, 6], [5, 5, 5, 5], [4, 4, 4, 0], [4, 4, 4, 0], [4, 4, 4, 0]]
 
 
 def tile_coil_compress_regrid_d4_kernel(tc, x_bytes, x_scale, c, o, w, e_words, e_scales, out):
@@ -53,6 +53,7 @@ def tile_coil_compress_regrid_d4_kernel(tc, x_bytes, x_scale, c, o, w, e_words, 
         e_codes = ring(GROUPS, [P, 2 * G], U8, "e_codes")
         e_exps = sb.tile([P, GROUPS, G], U8, name="e_exps", align_bytes=64)
         o_row = sb.tile([P, V], BF16, name="o_row")
+        zeros = sb.tile([P, BANK], BF16, name="zeros")
         ones = sb.tile([P, P], BF16, name="ones")
         o_all = sb.tile([P, V], F32, name="o_all")
         ident = sb.tile([P, P], F32, name="ident")
@@ -85,10 +86,10 @@ def tile_coil_compress_regrid_d4_kernel(tc, x_bytes, x_scale, c, o, w, e_words, 
         def load_e(g):
             nc.sync.dma_start(out=e_codes[g][:].bitcast(I32), in_=e_words[g].bitcast(I32))
 
+        nc.vector.memset(zeros[:], 0.0)
         nc.vector.memset(o_row[:], 0.0)
-        nc.vector.memset(ones[:], 0.0)
         nc.vector.memset(e_exps[:].rearrange("p g n -> p (g n)").bitcast(I32), 0)
-        nc.scalar.activation(out=ones[:], in_=ones[:], func=COPY, bias=1.0)
+        nc.scalar.activation(out=ones[:], in_=zeros[:, :P], func=COPY, bias=1.0)
         make_identity(nc, ident[:])
 
         nc.sync.dma_start(out=x_raw[0][:, : 2 * K], in_=x_rows[0][:, : 2 * K])
@@ -117,9 +118,14 @@ def tile_coil_compress_regrid_d4_kernel(tc, x_bytes, x_scale, c, o, w, e_words, 
 
         def widen_block(g, t, b, on_vector):
             src = x_raw[g][:, t * K + b * BLOCK : t * K + (b + 1) * BLOCK].bitcast(FP8)
-            dst = x_wide[(PACK * g + t) % WIDE_BUFS][:, b * BLOCK : (b + 1) * BLOCK]
+            wide = x_wide[(PACK * g + t) % WIDE_BUFS]
+            dst = wide[:, b * BLOCK : (b + 1) * BLOCK]
             factor = x_factor[:, g, t * BLOCKS + b : t * BLOCKS + b + 1]
             if on_vector:
+                if b // PACK < VECTOR_BLOCKS[g][t] // PACK:
+                    s, q = divmod(b, PACK)
+                    dst = wide[:, s * PASS : (s + 1) * PASS].rearrange("p (u q m e) -> p q m u e", u=2, q=PACK, e=2)[:, q]
+                    src = src.rearrange("p (m u e) -> p m u e", u=2, e=2)
                 nc.vector.tensor_scalar(out=dst, in0=src, scalar1=factor, scalar2=None, op0=MULT)
             else:
                 nc.scalar.activation(out=dst, in_=src, func=COPY, scale=factor)
@@ -139,7 +145,10 @@ def tile_coil_compress_regrid_d4_kernel(tc, x_bytes, x_scale, c, o, w, e_words, 
             for s in range(K_PASSES):
                 for u in range(2):
                     col = (2 * s + u) * P
-                    nc.tensor.transpose(bank[:, col : col + P], words[:, 2 * P * s + u : 2 * P * (s + 1) : 2], ident[:])
+                    if s < VECTOR_BLOCKS[g][t] // PACK:
+                        nc.tensor.transpose(bank[:, col : col + P], words[:, col : col + P], ident[:])
+                    else:
+                        nc.tensor.transpose(bank[:, col : col + P], words[:, 2 * P * s + u : 2 * P * (s + 1) : 2], ident[:])
 
         def empty_turned(g, t, bank):
             dst = x_turned[(2 * g + t // 2) % TURNED_BUFS][:, (t % 2) * K : (t % 2 + 1) * K].bitcast(F32)
@@ -192,20 +201,23 @@ def tile_coil_compress_regrid_d4_kernel(tc, x_bytes, x_scale, c, o, w, e_words, 
                 op=SUBTRACT,
             )
 
-        def weigh(g, half):
+        def weigh(g, half, first=0, count=HALF):
+            cols = slice(first, first + count)
+            w_cols = slice(half * HALF + first, half * HALF + first + count)
             nc.vector.tensor_tensor(
-                out=h_grouped[g % 2][:].rearrange("p (a b) t -> p a t b", b=PACK),
-                in0=shifted[g % 2][:].rearrange("p t (a b) -> p a t b", b=PACK),
-                in1=w_raw[g][:, :, half * HALF : (half + 1) * HALF].rearrange("p t (a b) -> p a t b", b=PACK),
+                out=h_grouped[g % 2][:, cols, :].rearrange("p (a b) t -> p a t b", b=PACK),
+                in0=shifted[g % 2][:, :, cols].rearrange("p t (a b) -> p a t b", b=PACK),
+                in1=w_raw[g][:, :, w_cols].rearrange("p t (a b) -> p a t b", b=PACK),
                 op=MULT,
             )
 
-        def quantize_h(g, half):
+        def quantize_h(g, half, first=0, count=HALF):
             n = 2 * g + half
+            cols = slice(first, first + count)
             nc.vector.quantize_mx(
-                out=h_codes[n][:].bitcast(FP8X4),
-                scales=h_exps[n][:],
-                in_=h_grouped[g % 2][:].rearrange("p v t -> p (v t)"),
+                out=h_codes[n][:, cols].bitcast(FP8X4),
+                scales=h_exps[n][:, cols],
+                in_=h_grouped[g % 2][:, cols, :].rearrange("p v t -> p (v t)"),
             )
 
         def regrid(g, row, col, bank):
@@ -252,7 +264,11 @@ def tile_coil_compress_regrid_d4_kernel(tc, x_bytes, x_scale, c, o, w, e_words, 
             for row, col, bank in tiles:
                 regrid(g, row, col, bank)
 
-        nc.tensor.matmul(out=sums[0][:], lhsT=ones[:], rhs=o_row[:], start=True, stop=True)
+        def keep_warm(count):
+            for i in range(count):
+                nc.tensor.matmul(out=sums[1][:], lhsT=zeros[:, :P], rhs=zeros[:], start=True, stop=True)
+
+        keep_warm(5)
         for t in range(PACK):
             widen_vector(0, t)
             widen_scalar(0, t)
@@ -262,6 +278,9 @@ def tile_coil_compress_regrid_d4_kernel(tc, x_bytes, x_scale, c, o, w, e_words, 
         group_c(0, 1, True)
         for t in range(PACK):
             turn(0, t, turned[t])
+            if t == 1:
+                nc.tensor.matmul(out=sums[0][:], lhsT=ones[:], rhs=o_row[:], start=True, stop=True)
+            keep_warm(1)
             empty_turned(0, t, turned[t])
             widen_vector(1, t)
             if t == 0:
@@ -274,101 +293,85 @@ def tile_coil_compress_regrid_d4_kernel(tc, x_bytes, x_scale, c, o, w, e_words, 
         widen_scalar(1, 3)
 
         for g in range(GROUPS - 1):
-            turned = [next_bank() for t in range(PACK)]
+            turned = [next_bank(), next_bank()]
+            made = [next_bank(), next_bank()]
+            turned.extend([next_bank(), next_bank()])
             quantize_x(g, 1)
             turn(g + 1, 0, turned[0])
+            turn(g + 1, 1, turned[1])
+            compress_both(g, 0, made)
             widen_scalar(g + 2, 0)
-            if g == GROUPS - 2:
-                group_c(1, 0, False)
+            empty_turned(g + 1, 0, turned[0])
+            empty_turned(g + 1, 1, turned[1])
             if g >= 1:
                 weigh(g - 1, 0)
-            empty_turned(g + 1, 0, turned[0])
-            turn(g + 1, 1, turned[1])
             widen_vector(g + 2, 0)
-            if g == GROUPS - 2:
-                group_c(1, 1, True)
+            if g == 0:
+                widen_vector(g + 2, 1)
+                widen_vector(g + 2, 2)
             if g >= 1:
                 quantize_h(g - 1, 0)
-            widen_scalar(g + 2, 1)
-            empty_turned(g + 1, 1, turned[1])
-            widen_vector(g + 2, 1)
+            quantize_x(g + 1, 0)
             turn(g + 1, 2, turned[2])
             turn(g + 1, 3, turned[3])
-            quantize_x(g + 1, 0)
-            made = [next_bank(), next_bank()]
-            compress_both(g, 0, made)
+            widen_scalar(g + 2, 1)
             widen_scalar(g + 2, 2)
             empty_turned(g + 1, 2, turned[2])
-            widen_vector(g + 2, 2)
-            if g == GROUPS - 2:
-                quantize_c(1)
-            shift_both(g, 0, made)
-            widen_scalar(g + 2, 3)
             empty_turned(g + 1, 3, turned[3])
+            widen_scalar(g + 2, 3)
+            shift_both(g, 0, made)
+            if g >= 1:
+                widen_vector(g + 2, 1)
+                widen_vector(g + 2, 2)
             widen_vector(g + 2, 3)
+            if g == GROUPS - 2:
+                group_c(1, 0, False)
+                group_c(1, 1, False)
             if g >= 1:
                 regrid_all(g - 1, early)
+            else:
+                keep_warm(3)
 
         last = GROUPS - 1
-        odd, even = stream[2:], stream[:2]
+        extra = [(0, 2, turned[2]), (1, 2, turned[3])]
+        first_half = early + extra
+        second_half = [(2 + i // 3, i % 3, bank) for i, (row, col, bank) in enumerate(first_half)]
 
         quantize_x(last, 1)
         weigh(last - 1, 0)
-        compress_both(last, 0, odd)
-        shift(last, 0, 0, odd[0])
+        quantize_c(1)
+        compress(last, 0, 0, made[0])
+        regrid_all(0, extra)
+        compress(last, 0, 1, made[1])
+        for g in range(1, last - 1):
+            regrid_all(g, extra)
+        shift_both(last, 0, made)
         quantize_h(last - 1, 0)
-        compress_both(0, 1, even)
-        shift(last, 0, 1, odd[1])
-        regrid_all(last - 1, early)
-        shift(0, 1, 0, even[0])
         weigh(last, 0)
-        compress_both(1, 1, odd)
-        shift(0, 1, 1, even[1])
+        compress_both(0, 1, made)
+        regrid_all(last - 1, first_half)
+        shift_both(0, 1, made)
         quantize_h(last, 0)
-        compress_both(2, 1, even)
-        for row, col, bank in early:
+        weigh(0, 1)
+        compress_both(1, 1, made)
+        for row, col, bank in first_half:
             regrid(last, row, col, bank)
             store(row, col, bank, False)
-        weigh(0, 1)
-        shift_both(1, 1, odd)
-        quantize_h(0, 1)
-        weigh(1, 1)
-        compress_both(3, 1, odd)
-        for row in range(2):
-            for g in range(GROUPS):
-                regrid(g, row, 2, sums[row])
-            store(row, 2, sums[row], False)
-        shift_both(2, 1, even)
-        quantize_h(1, 1)
-        weigh(2, 1)
-        first_col = [(2, 0, sums[2]), (3, 0, sums[3])]
-        second_col = [(2, 1, sums[0]), (3, 1, sums[1])]
-        third_col = [(2, 2, odd[0]), (3, 2, odd[1])]
-        regrid_all(0, first_col)
-        regrid_all(1, first_col)
-        compress_both(4, 1, even)
-        regrid_all(0, second_col)
-        regrid_all(1, second_col)
-        shift_both(3, 1, odd)
-        quantize_h(2, 1)
-        weigh(3, 1)
-        regrid_all(2, first_col + second_col)
-        shift_both(4, 1, even)
-        quantize_h(3, 1)
-        weigh(4, 1)
-        compress_both(5, 1, even)
-        regrid_all(3, first_col + second_col)
-        shift_both(5, 1, even)
-        quantize_h(4, 1)
-        weigh(5, 1)
-        quantize_h(5, 1)
-        for g in range(3):
-            regrid_all(g, third_col)
-        regrid_all(4, first_col + second_col)
-        for i, (row, col, bank) in enumerate(first_col + second_col):
+        for g in range(1, last):
+            shift_both(g, 1, made)
+            quantize_h(g - 1, 1)
+            weigh(g, 1)
+            compress_both(g + 1, 1, made)
+            regrid_all(g - 1, second_half)
+        shift_both(last, 1, made)
+        quantize_h(last - 1, 1)
+        weigh(last, 1, 0, P)
+        quantize_h(last, 1, 0, P)
+        weigh(last, 1, P, P)
+        quantize_h(last, 1, P, P)
+        regrid_all(last - 1, second_half[:3])
+        for i, (row, col, bank) in enumerate(second_half):
+            if i >= 3:
+                regrid(last - 1, row, col, bank)
             regrid(last, row, col, bank)
-            store(row, col, bank, i % 2 == 1)
-        for i, (row, col, bank) in enumerate(third_col):
-            for g in range(3, GROUPS):
-                regrid(g, row, col, bank)
             store(row, col, bank, i % 2 == 1)

@@ -30,7 +30,7 @@ BANK = 512
 WIDE_BUFS = 8
 TURNED_BUFS = 3
 OUT_BUFS = 6
-VECTOR_BLOCKS = [[5, 5, 5, 5], [6, 6, 6, 6], [5, 5, 5, 5], [4, 4, 4, 0], [4, 4, 4, 0], [4, 4, 4, 0]]
+VECTOR_BLOCKS = [[5, 5, 5, 5], [6, 6, 6, 6], [5, 5, 5, 5], [4, 4, 4, 1], [4, 4, 4, 1], [4, 4, 4, 1]]
 
 
 def tile_coil_compress_regrid_d4_kernel(tc, x_bytes, x_scale, c, o, w, e_words, e_scales, out):
@@ -83,6 +83,14 @@ def tile_coil_compress_regrid_d4_kernel(tc, x_bytes, x_scale, c, o, w, e_words, 
             for s in range(K_PASSES):
                 nc.sync.dma_start(out=c_raw[half][:, s], in_=c_rows[s][:, :, half * HALF : (half + 1) * HALF])
 
+        def load_e_exps(part):
+            groups = slice(part * GROUPS // 2, (part + 1) * GROUPS // 2)
+            for q in range(4):
+                nc.sync.dma_start(
+                    out=e_exps[32 * q : 32 * q + 4, groups].bitcast(I32),
+                    in_=e_scales[groups, 4 * q : 4 * q + 4, :].bitcast(I32).rearrange("g r n -> r g n"),
+                )
+
         def load_e(g):
             nc.sync.dma_start(out=e_codes[g][:].bitcast(I32), in_=e_words[g].bitcast(I32))
 
@@ -92,26 +100,26 @@ def tile_coil_compress_regrid_d4_kernel(tc, x_bytes, x_scale, c, o, w, e_words, 
         nc.scalar.activation(out=ones[:], in_=zeros[:, :P], func=COPY, bias=1.0)
         make_identity(nc, ident[:])
 
-        nc.sync.dma_start(out=x_raw[0][:, : 2 * K], in_=x_rows[0][:, : 2 * K])
-        nc.sync.dma_start(out=x_factor[:], in_=x_scale.rearrange("(g p t) b -> p g (t b)", p=P, t=PACK))
-        nc.sync.dma_start(out=o_row[0:1, :], in_=o.rearrange("(a v) -> a v", a=1))
+        factors = x_scale.rearrange("(g p t) b -> p g (t b)", p=P, t=PACK)
+        nc.sync.dma_start(out=x_raw[0][:, :K], in_=x_rows[0][:, :K])
+        nc.sync.dma_start(out=x_factor[:, :1], in_=factors[:, :1])
+        nc.sync.dma_start(out=x_raw[0][:, K : 2 * K], in_=x_rows[0][:, K : 2 * K])
         nc.sync.dma_start(out=x_raw[0][:, 2 * K :], in_=x_rows[0][:, 2 * K :])
         load_c(0)
+        nc.sync.dma_start(out=o_row[0:1, :], in_=o.rearrange("(a v) -> a v", a=1))
+        nc.sync.dma_start(out=x_factor[:, 1:], in_=factors[:, 1:])
         load_x(1)
         load_x(2)
         load_w(0)
         load_x(3)
-        for q in range(4):
-            nc.sync.dma_start(
-                out=e_exps[32 * q : 32 * q + 4].bitcast(I32),
-                in_=e_scales[:, 4 * q : 4 * q + 4, :].bitcast(I32).rearrange("g r n -> r g n"),
-            )
+        load_e_exps(0)
         load_e(0)
         load_x(4)
         load_w(1)
         load_e(1)
         load_x(5)
         load_c(1)
+        load_e_exps(1)
         for g in range(2, GROUPS):
             load_w(g)
             load_e(g)
@@ -235,14 +243,18 @@ def tile_coil_compress_regrid_d4_kernel(tc, x_bytes, x_scale, c, o, w, e_words, 
 
         stored = []
 
-        def store(row, col, bank, on_vector):
+        def store(row, col, bank, on_vector, pieces=1):
             stage = z_stage[len(stored) % OUT_BUFS]
             stored.append((row, col))
-            if on_vector:
-                nc.vector.tensor_copy(out=stage[:], in_=bank[:])
-            else:
-                nc.scalar.copy(out=stage[:], in_=bank[:])
-            nc.sync.dma_start(out=out[row * P : (row + 1) * P, col * BANK : (col + 1) * BANK], in_=stage[:])
+            width = BANK // pieces
+            for first in range(0, BANK, width):
+                cols = slice(first, first + width)
+                if on_vector:
+                    nc.vector.tensor_copy(out=stage[:, cols], in_=bank[:, cols])
+                else:
+                    nc.scalar.copy(out=stage[:, cols], in_=bank[:, cols])
+                z_cols = slice(col * BANK + first, col * BANK + first + width)
+                nc.sync.dma_start(out=out[row * P : (row + 1) * P, z_cols], in_=stage[:, cols])
 
         taken = []
 
@@ -268,7 +280,7 @@ def tile_coil_compress_regrid_d4_kernel(tc, x_bytes, x_scale, c, o, w, e_words, 
             for i in range(count):
                 nc.tensor.matmul(out=sums[1][:], lhsT=zeros[:, :P], rhs=zeros[:], start=True, stop=True)
 
-        keep_warm(5)
+        keep_warm(4)
         for t in range(PACK):
             widen_vector(0, t)
             widen_scalar(0, t)
@@ -330,7 +342,7 @@ def tile_coil_compress_regrid_d4_kernel(tc, x_bytes, x_scale, c, o, w, e_words, 
             if g >= 1:
                 regrid_all(g - 1, early)
             else:
-                keep_warm(3)
+                keep_warm(2)
 
         last = GROUPS - 1
         extra = [(0, 2, turned[2]), (1, 2, turned[3])]
@@ -374,4 +386,4 @@ def tile_coil_compress_regrid_d4_kernel(tc, x_bytes, x_scale, c, o, w, e_words, 
             if i >= 3:
                 regrid(last - 1, row, col, bank)
             regrid(last, row, col, bank)
-            store(row, col, bank, i % 2 == 1)
+            store(row, col, bank, i % 2 == 1, 2 if i == 5 else 1)

from contextlib import ExitStack

import concourse.mybir as mybir
from concourse.masks import make_identity

T, K, V, G = 3072, 1024, 512, 1536
FLOPS = 2 * T * K * V + 2 * V * T * G

F32 = mybir.dt.float32
BF16 = mybir.dt.bfloat16
I32 = mybir.dt.int32
U32 = mybir.dt.uint32
U8 = mybir.dt.uint8
FP8 = mybir.dt.float8_e4m3fn
FP8X4 = mybir.dt.float8_e4m3fn_x4
FP4X4 = mybir.dt.float4_e2m1fn_x4
MULT = mybir.AluOpType.mult
SUBTRACT = mybir.AluOpType.subtract
COPY = mybir.ActivationFunctionType.Copy

P = 128
PACK = 4
PASS = P * PACK
GROUPS = T // PASS
K_PASSES = K // PASS
BLOCK = 128
BLOCKS = K // BLOCK
HALF = V // 2
BANK = 512
WIDE_BUFS = 8
TURNED_BUFS = 3
OUT_BUFS = 6
VECTOR_BLOCKS = [[5, 5, 5, 5], [6, 6, 6, 6], [5, 5, 5, 5], [4, 4, 4, 1], [4, 4, 4, 1], [4, 4, 4, 1]]


def tile_coil_compress_regrid_d4_kernel(tc, x_bytes, x_scale, c, o, w, e_words, e_scales, out):
    nc = tc.nc
    with ExitStack() as ctx:
        sb = ctx.enter_context(tc.tile_pool(name="sb", bufs=1))
        ps = ctx.enter_context(tc.psum_pool(name="ps", bufs=1))
        ctx.enter_context(tc.manual_schedule())

        def ring(count, shape, dtype, name):
            return [sb.tile(shape, dtype, name="%s%d" % (name, i), align_bytes=64) for i in range(count)]

        x_raw = ring(GROUPS, [P, PACK * K], U8, "x_raw")
        x_factor = sb.tile([P, GROUPS, PACK * BLOCKS], F32, name="x_factor")
        c_raw = ring(2, [P, K_PASSES, PACK, HALF], BF16, "c_raw")
        c_grouped = ring(2, [P, K_PASSES, HALF, PACK], BF16, "c_grouped")
        c_codes = ring(2, [P, K_PASSES * HALF], U32, "c_codes")
        c_exps = ring(2, [P, K_PASSES * HALF], U8, "c_exps")
        w_raw = ring(GROUPS, [P, PACK, V], BF16, "w_raw")
        e_codes = ring(GROUPS, [P, 2 * G], U8, "e_codes")
        e_exps = sb.tile([P, GROUPS, G], U8, name="e_exps", align_bytes=64)
        o_row = sb.tile([P, V], BF16, name="o_row")
        zeros = sb.tile([P, BANK], BF16, name="zeros")
        ones = sb.tile([P, P], BF16, name="ones")
        o_all = sb.tile([P, V], F32, name="o_all")
        ident = sb.tile([P, P], F32, name="ident")
        x_wide = ring(WIDE_BUFS, [P, K], BF16, "x_wide")
        x_turned = ring(TURNED_BUFS, [P, 2 * K], BF16, "x_turned")
        x_codes = ring(2 * GROUPS, [P, 2 * K // PACK], U32, "x_codes")
        x_exps = ring(2 * GROUPS, [P, 2 * K // PACK], U8, "x_exps")
        shifted = ring(2, [P, PACK, HALF], F32, "shifted")
        h_grouped = ring(2, [P, HALF, PACK], BF16, "h_grouped")
        h_codes = ring(2 * GROUPS, [P, HALF], U32, "h_codes")
        h_exps = ring(2 * GROUPS, [P, HALF], U8, "h_exps")
        z_stage = ring(OUT_BUFS, [P, BANK], F32, "z_stage")
        banks = [ps.tile([P, BANK], F32, name="bank%d" % i) for i in range(8)]
        sums, stream = banks[:4], banks[4:]

        x_rows = x_bytes.rearrange("(g p t) k -> g p (t k)", p=P, t=PACK)
        w_rows = w.rearrange("(g p t) v -> g p t v", p=P, t=PACK)
        c_rows = c.rearrange("(s p j) v -> s p j v", p=P, j=PACK)

        def load_x(g):
            nc.sync.dma_start(out=x_raw[g][:], in_=x_rows[g])

        def load_w(g):
            nc.sync.dma_start(out=w_raw[g][:], in_=w_rows[g])

        def load_c(half):
            for s in range(K_PASSES):
                nc.sync.dma_start(out=c_raw[half][:, s], in_=c_rows[s][:, :, half * HALF : (half + 1) * HALF])

        def load_e_exps(part):
            groups = slice(part * GROUPS // 2, (part + 1) * GROUPS // 2)
            for q in range(4):
                nc.sync.dma_start(
                    out=e_exps[32 * q : 32 * q + 4, groups].bitcast(I32),
                    in_=e_scales[groups, 4 * q : 4 * q + 4, :].bitcast(I32).rearrange("g r n -> r g n"),
                )

        def load_e(g):
            nc.sync.dma_start(out=e_codes[g][:].bitcast(I32), in_=e_words[g].bitcast(I32))

        nc.vector.memset(zeros[:], 0.0)
        nc.vector.memset(o_row[:], 0.0)
        nc.vector.memset(e_exps[:].rearrange("p g n -> p (g n)").bitcast(I32), 0)
        nc.scalar.activation(out=ones[:], in_=zeros[:, :P], func=COPY, bias=1.0)
        make_identity(nc, ident[:])

        factors = x_scale.rearrange("(g p t) b -> p g (t b)", p=P, t=PACK)
        nc.sync.dma_start(out=x_raw[0][:, :K], in_=x_rows[0][:, :K])
        nc.sync.dma_start(out=x_factor[:, :1], in_=factors[:, :1])
        nc.sync.dma_start(out=x_raw[0][:, K : 2 * K], in_=x_rows[0][:, K : 2 * K])
        nc.sync.dma_start(out=x_raw[0][:, 2 * K :], in_=x_rows[0][:, 2 * K :])
        load_c(0)
        nc.sync.dma_start(out=o_row[0:1, :], in_=o.rearrange("(a v) -> a v", a=1))
        nc.sync.dma_start(out=x_factor[:, 1:], in_=factors[:, 1:])
        load_x(1)
        load_x(2)
        load_w(0)
        load_x(3)
        load_e_exps(0)
        load_e(0)
        load_x(4)
        load_w(1)
        load_e(1)
        load_x(5)
        load_c(1)
        load_e_exps(1)
        for g in range(2, GROUPS):
            load_w(g)
            load_e(g)

        def widen_block(g, t, b, on_vector):
            src = x_raw[g][:, t * K + b * BLOCK : t * K + (b + 1) * BLOCK].bitcast(FP8)
            wide = x_wide[(PACK * g + t) % WIDE_BUFS]
            dst = wide[:, b * BLOCK : (b + 1) * BLOCK]
            factor = x_factor[:, g, t * BLOCKS + b : t * BLOCKS + b + 1]
            if on_vector:
                if b // PACK < VECTOR_BLOCKS[g][t] // PACK:
                    s, q = divmod(b, PACK)
                    dst = wide[:, s * PASS : (s + 1) * PASS].rearrange("p (u q m e) -> p q m u e", u=2, q=PACK, e=2)[:, q]
                    src = src.rearrange("p (m u e) -> p m u e", u=2, e=2)
                nc.vector.tensor_scalar(out=dst, in0=src, scalar1=factor, scalar2=None, op0=MULT)
            else:
                nc.scalar.activation(out=dst, in_=src, func=COPY, scale=factor)

        def widen_vector(g, t):
            if g < GROUPS:
                for b in range(VECTOR_BLOCKS[g][t]):
                    widen_block(g, t, b, True)

        def widen_scalar(g, t):
            if g < GROUPS:
                for b in range(VECTOR_BLOCKS[g][t], BLOCKS):
                    widen_block(g, t, b, False)

        def turn(g, t, bank):
            words = x_wide[(PACK * g + t) % WIDE_BUFS][:].bitcast(F32)
            for s in range(K_PASSES):
                for u in range(2):
                    col = (2 * s + u) * P
                    if s < VECTOR_BLOCKS[g][t] // PACK:
                        nc.tensor.transpose(bank[:, col : col + P], words[:, col : col + P], ident[:])
                    else:
                        nc.tensor.transpose(bank[:, col : col + P], words[:, 2 * P * s + u : 2 * P * (s + 1) : 2], ident[:])

        def empty_turned(g, t, bank):
            dst = x_turned[(2 * g + t // 2) % TURNED_BUFS][:, (t % 2) * K : (t % 2 + 1) * K].bitcast(F32)
            nc.scalar.copy(
                out=dst.rearrange("p (s r u) -> p s r u", s=K_PASSES, u=2),
                in_=bank[:].rearrange("p (s u r) -> p s r u", s=K_PASSES, u=2),
            )

        def quantize_x(g, pair):
            n = 2 * g + pair
            nc.vector.quantize_mx(out=x_codes[n][:].bitcast(FP8X4), scales=x_exps[n][:], in_=x_turned[n % TURNED_BUFS][:])

        def group_c(half, s, on_vector):
            src = c_raw[half][:, s].rearrange("p j (a b) -> p a j b", b=PACK)
            dst = c_grouped[half][:, s].rearrange("p (a b) j -> p a j b", b=PACK)
            if on_vector:
                nc.vector.tensor_copy(out=dst, in_=src)
            else:
                nc.scalar.copy(out=dst, in_=src)

        def quantize_c(half):
            nc.vector.quantize_mx(
                out=c_codes[half][:].bitcast(FP8X4),
                scales=c_exps[half][:],
                in_=c_grouped[half][:].rearrange("p s v j -> p (s v j)"),
            )

        def compress(g, half, pair, bank):
            n = 2 * g + pair
            for slot in range(2):
                for s in range(K_PASSES):
                    cols = slice((slot * K_PASSES + s) * P, (slot * K_PASSES + s + 1) * P)
                    c_cols = slice(s * HALF, (s + 1) * HALF)
                    nc.tensor.matmul_mx(
                        out=bank[:, slot * HALF : (slot + 1) * HALF],
                        lhsT=x_codes[n][:, cols].bitcast(FP8X4),
                        lhsT_scale=x_exps[n][:, cols],
                        rhs=c_codes[half][:, c_cols].bitcast(FP8X4),
                        rhs_scale=c_exps[half][:, c_cols],
                        start=(s == 0),
                        stop=(s == K_PASSES - 1),
                    )

        def shift(g, half, pair, bank):
            offset = o_all[:, half * HALF : (half + 1) * HALF].unsqueeze(1).to_broadcast([P, 2, HALF])
            nc.vector.tensor_tensor(
                out=shifted[g % 2][:, 2 * pair : 2 * pair + 2, :],
                in0=bank[:].rearrange("p (t v) -> p t v", t=2),
                in1=offset,
                op=SUBTRACT,
            )

        def weigh(g, half, first=0, count=HALF):
            cols = slice(first, first + count)
            w_cols = slice(half * HALF + first, half * HALF + first + count)
            nc.vector.tensor_tensor(
                out=h_grouped[g % 2][:, cols, :].rearrange("p (a b) t -> p a t b", b=PACK),
                in0=shifted[g % 2][:, :, cols].rearrange("p t (a b) -> p a t b", b=PACK),
                in1=w_raw[g][:, :, w_cols].rearrange("p t (a b) -> p a t b", b=PACK),
                op=MULT,
            )

        def quantize_h(g, half, first=0, count=HALF):
            n = 2 * g + half
            cols = slice(first, first + count)
            nc.vector.quantize_mx(
                out=h_codes[n][:, cols].bitcast(FP8X4),
                scales=h_exps[n][:, cols],
                in_=h_grouped[g % 2][:, cols, :].rearrange("p v t -> p (v t)"),
            )

        def regrid(g, row, col, bank):
            n = 2 * g + row // 2
            cols = slice((row % 2) * P, (row % 2 + 1) * P)
            nc.tensor.matmul_mx(
                out=bank[:],
                lhsT=h_codes[n][:, cols].bitcast(FP8X4),
                lhsT_scale=h_exps[n][:, cols],
                rhs=e_codes[g][:, 2 * col * BANK : 2 * (col + 1) * BANK].bitcast(FP4X4),
                rhs_scale=e_exps[:, g, col * BANK : (col + 1) * BANK],
                start=(g == 0),
                stop=(g == GROUPS - 1),
            )

        stored = []

        def store(row, col, bank, on_vector, pieces=1):
            stage = z_stage[len(stored) % OUT_BUFS]
            stored.append((row, col))
            width = BANK // pieces
            for first in range(0, BANK, width):
                cols = slice(first, first + width)
                if on_vector:
                    nc.vector.tensor_copy(out=stage[:, cols], in_=bank[:, cols])
                else:
                    nc.scalar.copy(out=stage[:, cols], in_=bank[:, cols])
                z_cols = slice(col * BANK + first, col * BANK + first + width)
                nc.sync.dma_start(out=out[row * P : (row + 1) * P, z_cols], in_=stage[:, cols])

        taken = []

        def next_bank():
            taken.append(0)
            return stream[(len(taken) - 1) % len(stream)]

        early = [(0, 0, sums[0]), (0, 1, sums[1]), (1, 0, sums[2]), (1, 1, sums[3])]

        def compress_both(g, half, pair_banks):
            compress(g, half, 0, pair_banks[0])
            compress(g, half, 1, pair_banks[1])

        def shift_both(g, half, pair_banks):
            shift(g, half, 0, pair_banks[0])
            shift(g, half, 1, pair_banks[1])

        def regrid_all(g, tiles):
            for row, col, bank in tiles:
                regrid(g, row, col, bank)

        def keep_warm(count):
            for i in range(count):
                nc.tensor.matmul(out=sums[1][:], lhsT=zeros[:, :P], rhs=zeros[:], start=True, stop=True)

        keep_warm(4)
        for t in range(PACK):
            widen_vector(0, t)
            widen_scalar(0, t)

        turned = [next_bank() for t in range(PACK)]
        group_c(0, 0, True)
        group_c(0, 1, True)
        for t in range(PACK):
            turn(0, t, turned[t])
            if t == 1:
                nc.tensor.matmul(out=sums[0][:], lhsT=ones[:], rhs=o_row[:], start=True, stop=True)
            keep_warm(1)
            empty_turned(0, t, turned[t])
            widen_vector(1, t)
            if t == 0:
                quantize_c(0)
            if t == 1:
                quantize_x(0, 0)
            if t >= 1:
                widen_scalar(1, t - 1)
        nc.scalar.copy(out=o_all[:], in_=sums[0][:])
        widen_scalar(1, 3)

        for g in range(GROUPS - 1):
            turned = [next_bank(), next_bank()]
            made = [next_bank(), next_bank()]
            turned.extend([next_bank(), next_bank()])
            quantize_x(g, 1)
            turn(g + 1, 0, turned[0])
            turn(g + 1, 1, turned[1])
            compress_both(g, 0, made)
            widen_scalar(g + 2, 0)
            empty_turned(g + 1, 0, turned[0])
            empty_turned(g + 1, 1, turned[1])
            if g >= 1:
                weigh(g - 1, 0)
            widen_vector(g + 2, 0)
            if g == 0:
                widen_vector(g + 2, 1)
                widen_vector(g + 2, 2)
            if g >= 1:
                quantize_h(g - 1, 0)
            quantize_x(g + 1, 0)
            turn(g + 1, 2, turned[2])
            turn(g + 1, 3, turned[3])
            widen_scalar(g + 2, 1)
            widen_scalar(g + 2, 2)
            empty_turned(g + 1, 2, turned[2])
            empty_turned(g + 1, 3, turned[3])
            widen_scalar(g + 2, 3)
            shift_both(g, 0, made)
            if g >= 1:
                widen_vector(g + 2, 1)
                widen_vector(g + 2, 2)
            widen_vector(g + 2, 3)
            if g == GROUPS - 2:
                group_c(1, 0, False)
                group_c(1, 1, False)
            if g >= 1:
                regrid_all(g - 1, early)
            else:
                keep_warm(2)

        last = GROUPS - 1
        extra = [(0, 2, turned[2]), (1, 2, turned[3])]
        first_half = early + extra
        second_half = [(2 + i // 3, i % 3, bank) for i, (row, col, bank) in enumerate(first_half)]

        quantize_x(last, 1)
        weigh(last - 1, 0)
        quantize_c(1)
        compress(last, 0, 0, made[0])
        regrid_all(0, extra)
        compress(last, 0, 1, made[1])
        for g in range(1, last - 1):
            regrid_all(g, extra)
        shift_both(last, 0, made)
        quantize_h(last - 1, 0)
        weigh(last, 0)
        compress_both(0, 1, made)
        regrid_all(last - 1, first_half)
        shift_both(0, 1, made)
        quantize_h(last, 0)
        weigh(0, 1)
        compress_both(1, 1, made)
        for row, col, bank in first_half:
            regrid(last, row, col, bank)
            store(row, col, bank, False)
        for g in range(1, last):
            shift_both(g, 1, made)
            quantize_h(g - 1, 1)
            weigh(g, 1)
            compress_both(g + 1, 1, made)
            regrid_all(g - 1, second_half)
        shift_both(last, 1, made)
        quantize_h(last - 1, 1)
        weigh(last, 1, 0, P)
        quantize_h(last, 1, 0, P)
        weigh(last, 1, P, P)
        quantize_h(last, 1, P, P)
        regrid_all(last - 1, second_half[:3])
        for i, (row, col, bank) in enumerate(second_half):
            if i >= 3:
                regrid(last - 1, row, col, bank)
            regrid(last, row, col, bank)
            store(row, col, bank, i % 2 == 1, 2 if i == 5 else 1)
